import numpy as np
import ml_dtypes


def mxq(x, axis, fmt="e4m3"):
    dtype, down = {"e4m3": (ml_dtypes.float8_e4m3fn, 7), "e5m2": (ml_dtypes.float8_e5m2, 14)}[fmt]
    v = np.moveaxis(np.asarray(x, np.float32).astype(ml_dtypes.bfloat16).astype(np.float64), axis, -1)
    blocks = v.reshape(v.shape[:-1] + (-1, 32))
    amax = np.abs(blocks).max(-1, keepdims=True)
    byte = np.maximum(np.where(amax > 0, np.frexp(amax)[1] - 1 + 127, 0) - down, 1)
    scale = np.exp2(byte - 127.0)
    codes = (blocks / scale).astype(np.float32).astype(dtype).astype(np.float64)
    return np.moveaxis((codes * scale).reshape(v.shape), -1, axis)


WIDE = False


def mx_kscale(k):
    if not WIDE:
        return np.ones(k)
    levels = np.array([10, -10, 5, -5, 0])
    if k % 512:
        return np.exp2(np.random.permutation(np.resize(levels, k // 32))).repeat(32)
    a = np.empty((k // 512, 16))
    for p in range(k // 512):
        a[p, :8] = np.random.permutation(np.resize(levels, 8))
        for g in range(8):
            far = levels[np.abs(levels - a[p, g]) >= 10]
            a[p, g + 8] = far[np.random.randint(len(far))]
    return np.exp2(a.ravel()).repeat(32)


def f64(x):
    return np.asarray(x).astype(np.float64)


def striped(idx):
    return np.tile(idx.reshape(-1, 16).T, (8, 1)).astype(np.uint16)


def unstriped(offs):
    return offs[:16].T.reshape(-1).astype(np.int64)


def pack_weight(w):
    k, n = w.shape
    w = f64(np.asarray(w, np.float32).astype(ml_dtypes.bfloat16)).reshape(k // 32, 32, n)
    amax = np.abs(w).max(1)
    byte = np.clip(np.where(amax > 0, np.frexp(amax)[1] - 1 + 127 - 7, 1), 1, 254)
    scaled = (w * np.exp2(127.0 - byte)[:, None, :]).reshape(k, n).astype(np.float32)
    words = np.ascontiguousarray(scaled.reshape(k // 512, 128, 4, n).transpose(0, 1, 3, 2)).astype(ml_dtypes.float8_e4m3fn).view(np.uint8)
    return words, np.ascontiguousarray(byte.astype(np.uint8).reshape(k // 512, 16, n))


def unpack_weight(words, scales):
    g, p, n, _ = words.shape
    vals = np.ascontiguousarray(words).view(ml_dtypes.float8_e4m3fn).astype(np.float64) * np.repeat(np.exp2(scales.astype(np.float64) - 127.0), 8, axis=1)[..., None]
    return vals.transpose(0, 1, 3, 2).reshape(g * 512, n)


def sigmoid(v):
    return 1.0 / (1.0 + np.exp(-np.maximum(v, -700.0)))


K, T, S, N, H = 512, 2048, 256, 512, 512


def setup_inputs():
    n = np.random.standard_normal
    s = mx_kscale(K)[:, None]
    u = mx_kscale(H)
    packed_xT = pack_weight(n((K, T)) * s)
    return {
        "x_words": packed_xT[0],
        "x_scales": packed_xT[1],
        "w1": (n((K, H)) / np.sqrt(K) / s).astype(np.float32),
        "gn": (np.random.uniform(0.5, 1.5, (H, 1)) * u[:, None]).astype(np.float32),
        "w2": (n((H, N)) / np.sqrt(H) / u[:, None]).astype(np.float32),
        "sl": np.random.uniform(1.0, 2.0, (H, 1)).astype(np.float32),
        "th": (0.5 * n((H, 1))).astype(np.float32),
        "offs": striped(np.random.permutation(T)[:S]),
        "n1": striped(np.random.permutation(S)),
        "n2": striped(np.random.permutation(S)),
        "n3": striped(np.random.permutation(S)),
        "n4": striped(np.random.permutation(S)),
        "n5": striped(np.random.permutation(S)),
    }


def reference(x_words, x_scales, w1, gn, w2, sl, th, offs, n1, n2, n3, n4, n5):
    xq = unpack_weight(x_words, x_scales)[:, unstriped(offs)]
    y = mxq(f64(w1), 0, "e4m3").T @ xq
    pa = y[:, unstriped(n1)]
    z = f64(gn) * (pa + (sigmoid(y[:, unstriped(n2)])) * (y[:, unstriped(n3)] - pa))
    h = mxq(f64(w2), 0, "e4m3").T @ mxq(z, 0, "e4m3")
    sg = sigmoid(f64(sl) * (y[:, unstriped(n4)] - f64(th)))
    return np.maximum(h * sg, y[:, unstriped(n5)] - y)

@@ -1,0 +1,185 @@
+from contextlib import ExitStack
+
+import concourse.mybir as mybir
+
+K, T, S, H, N = 512, 2048, 256, 512, 512
+FLOPS = 2 * K * H * S + 2 * H * N * S
+
+F32 = mybir.dt.float32
+BF16 = mybir.dt.bfloat16
+I32 = mybir.dt.int32
+U32 = mybir.dt.uint32
+U16 = mybir.dt.uint16
+U8 = mybir.dt.uint8
+FP8X4 = mybir.dt.float8_e4m3fn_x4
+ALU = mybir.AluOpType
+ACT = mybir.ActivationFunctionType
+
+P = 128
+PACK = 4
+HALF = S // 2
+LIST_COLS = S // 16
+W1_VECTOR_SHARE = 88
+
+
+def deal(engine_copy, grouped, raw, m0, m1):
+    engine_copy(
+        grouped[:].rearrange("p (t m j) -> p m j t", t=PACK, j=PACK)[:, m0:m1],
+        raw[:].rearrange("p j (m t) -> p m j t", t=PACK)[:, m0:m1],
+    )
+
+
+def tile_picked_skipmxblerp_none_p_kernel(
+    tc, x_words, x_scales, w1, gn, w2, sl, th, offs, n1, n2, n3, n4, n5, out
+):
+    nc = tc.nc
+    with ExitStack() as ctx:
+        keep = ctx.enter_context(tc.tile_pool(name="keep", bufs=1))
+        psum = ctx.enter_context(tc.psum_pool(name="psum", bufs=1))
+
+        w1_raw = keep.tile([P, PACK, H], F32, name="w1_raw")
+        nc.sync.dma_start(w1_raw[:], w1.rearrange("(p j) c -> p j c", j=PACK))
+        offs_t = keep.tile([P, LIST_COLS], U16, name="offs_t")
+        nc.sync.dma_start(offs_t[:], offs)
+        x_tab = keep.tile([P, T], U32, name="x_tab")
+        nc.sync.dma_start(x_tab[:].bitcast(I32), x_words[0].rearrange("p n t -> p (n t)").bitcast(I32))
+
+        s_tab = keep.tile([P, T], U8, name="s_tab")
+        nc.vector.memset(s_tab[:].bitcast(I32), 0)
+        for q in range(4):
+            nc.scalar.dma_start(
+                s_tab[32 * q : 32 * q + 4, :].bitcast(I32), x_scales[0, 4 * q : 4 * q + 4, :].bitcast(I32)
+            )
+
+        lists = {}
+        for name, src in (("n2", n2), ("n1", n1), ("n3", n3), ("n5", n5), ("n4", n4)):
+            lists[name] = keep.tile([P, LIST_COLS], U16, name=name + "_t")
+            nc.sync.dma_start(lists[name][:], src)
+        w2_raw = keep.tile([P, PACK, N], F32, name="w2_raw")
+        nc.sync.dma_start(w2_raw[:], w2.rearrange("(p j) c -> p j c", j=PACK))
+
+        cols = {}
+        for name, src in (("gn", gn), ("sl", sl), ("th", th)):
+            cols[name] = keep.tile([P, PACK], F32, name=name + "_t")
+            nc.gpsimd.dma_start(cols[name][:], src.rearrange("(p t) o -> p (t o)", t=PACK))
+
+        xg_scales = keep.tile([P, S], U8, name="xg_scales", align_bytes=64)
+        nc.vector.tensor_copy(xg_scales[:], s_tab[:].indirect(offs_t[:]))
+
+        w1_bf = keep.tile([P, PACK * H], BF16, name="w1_bf", align_bytes=64)
+        deal(nc.vector.tensor_copy, w1_bf, w1_raw, 0, W1_VECTOR_SHARE)
+        deal(nc.scalar.copy, w1_bf, w1_raw, W1_VECTOR_SHARE, P)
+        w1_codes = keep.tile([P, H], U32, name="w1_codes", align_bytes=64)
+        w1_scales = keep.tile([P, H], U8, name="w1_scales", align_bytes=64)
+        nc.vector.quantize_mx(out=w1_codes[:].bitcast(FP8X4), scales=w1_scales[:], in_=w1_bf[:])
+
+        bias = keep.tile([P, PACK], F32, name="bias")
+        sl_th = keep.tile([P, PACK], F32, name="sl_th")
+        nc.gpsimd.tensor_tensor(sl_th[:], cols["sl"][:], cols["th"][:], ALU.mult)
+        nc.gpsimd.tensor_scalar(bias[:], sl_th[:], -1.0, 0.0, ALU.mult, ALU.add)
+
+        xg_words = keep.tile([P, S], U32, name="xg_words", align_bytes=64)
+        nc.vector.tensor_copy(xg_words[:], x_tab[:].indirect(offs_t[:]))
+
+        y = []
+        y_twin = []
+        for t in range(PACK):
+            y_bank = psum.tile([P, S], F32, name="y_bank%d" % t)
+            m_cols = slice(t * P, (t + 1) * P)
+            nc.tensor.matmul_mx(
+                out=y_bank[:],
+                lhsT=w1_codes[:, m_cols].bitcast(FP8X4),
+                lhsT_scale=w1_scales[:, m_cols],
+                rhs=xg_words[:].bitcast(FP8X4),
+                rhs_scale=xg_scales[:],
+                start=True,
+                stop=True,
+            )
+            y.append(keep.tile([P, S], F32, name="y%d" % t))
+            nc.vector.tensor_copy(y[t][:], y_bank[:])
+            y_twin.append(keep.tile([P, S], F32, name="y_twin%d" % t))
+            nc.sync.dma_start(y_twin[t][:], y[t][:])
+
+        w2_bf = keep.tile([P, PACK * N], BF16, name="w2_bf", align_bytes=64)
+        deal(nc.vector.tensor_copy, w2_bf, w2_raw, 0, P)
+        w2_codes = keep.tile([P, N], U32, name="w2_codes", align_bytes=64)
+        w2_scales = keep.tile([P, N], U8, name="w2_scales", align_bytes=64)
+        nc.vector.quantize_mx(out=w2_codes[:].bitcast(FP8X4), scales=w2_scales[:], in_=w2_bf[:])
+
+        def looked_up(t, name, half):
+            c0 = half * (LIST_COLS // 2)
+            return y[t][:].indirect(lists[name][:, c0 : c0 + LIST_COLS // 2])
+
+        def planes(name, half):
+            return keep.tile([P, PACK, HALF], F32, name="%s%d" % (name, half))
+
+        def second_product(half, gate_first):
+            pa, far, gate = planes("pa", half), planes("far", half), planes("gate", half)
+            for t in range(PACK):
+                if gate_first:
+                    nc.scalar.activation(gate[:, t, :], looked_up(t, "n2", half), ACT.Sigmoid)
+                nc.scalar.activation(pa[:, t, :], looked_up(t, "n1", half), ACT.Copy)
+                nc.scalar.activation(far[:, t, :], looked_up(t, "n3", half), ACT.Copy)
+            if not gate_first:
+                for t in range(PACK):
+                    nc.scalar.activation(gate[:, t, :], looked_up(t, "n2", half), ACT.Sigmoid)
+            step, z = planes("step", half), planes("z", half)
+            nc.vector.tensor_tensor(step[:], far[:], pa[:], ALU.subtract)
+            for t in range(PACK):
+                g = cols["gn"][:, t : t + 1]
+                nc.vector.scalar_tensor_tensor(far[:, t, :], step[:, t, :], g, gate[:, t, :], ALU.mult, ALU.mult)
+            for t in range(PACK):
+                g = cols["gn"][:, t : t + 1]
+                nc.vector.scalar_tensor_tensor(z[:, t, :], pa[:, t, :], g, far[:, t, :], ALU.mult, ALU.add)
+            z_bf = keep.tile([P, HALF * PACK], BF16, name="z_bf%d" % half, align_bytes=64)
+            nc.vector.tensor_copy(
+                z_bf[:].rearrange("p (c i t) -> p c t i", i=4, t=PACK),
+                z[:].rearrange("p t (c i) -> p c t i", i=4),
+            )
+            z_codes = keep.tile([P, HALF], U32, name="z_codes%d" % half, align_bytes=64)
+            z_scales = keep.tile([P, HALF], U8, name="z_scales%d" % half, align_bytes=64)
+            nc.vector.quantize_mx(out=z_codes[:].bitcast(FP8X4), scales=z_scales[:], in_=z_bf[:])
+            h_bank = psum.tile([P, PACK, HALF], F32, name="h_bank%d" % half)
+            for t in range(PACK):
+                m_cols = slice(t * P, (t + 1) * P)
+                nc.tensor.matmul_mx(
+                    out=h_bank[:, t, :],
+                    lhsT=w2_codes[:, m_cols].bitcast(FP8X4),
+                    lhsT_scale=w2_scales[:, m_cols],
+                    rhs=z_codes[:].bitcast(FP8X4),
+                    rhs_scale=z_scales[:],
+                    start=True,
+                    stop=True,
+                )
+            return h_bank
+
+        def skip(half):
+            diff = planes("diff", half)
+            for t in range(PACK):
+                nc.vector.tensor_tensor(
+                    diff[:, t, :], looked_up(t, "n5", half), y_twin[t][:, half * HALF : (half + 1) * HALF], ALU.subtract
+                )
+            return diff
+
+        out_v = out.rearrange("(p t) j -> p t j", t=PACK)
+
+        def finish(half, h_bank, diff, pieces):
+            sg = planes("sg", half)
+            for t in range(PACK):
+                nc.scalar.activation(
+                    sg[:, t, :], looked_up(t, "n4", half), ACT.Sigmoid,
+                    bias=bias[:, t : t + 1], scale=cols["sl"][:, t : t + 1],
+                )
+            gated, res = planes("gated", half), planes("res", half)
+            for piece in pieces:
+                nc.vector.tensor_tensor(gated[:, piece, :], h_bank[:, piece, :], sg[:, piece, :], ALU.mult)
+            for piece in pieces:
+                nc.vector.tensor_tensor(res[:, piece, :], gated[:, piece, :], diff[:, piece, :], ALU.max)
+                nc.sync.dma_start(out_v[:, piece, half * HALF : (half + 1) * HALF], res[:, piece, :])
+
+        h0 = second_product(0, True)
+        d0 = skip(0)
+        h1 = second_product(1, False)
+        d1 = skip(1)
+        finish(0, h0, d0, [slice(0, 4)])
+        finish(1, h1, d1, [slice(0, 2), slice(2, 4)])

@@ -37,10 +37,16 @@ def tile_picked_skipmxblerp_none_p_kernel(
         keep = ctx.enter_context(tc.tile_pool(name="keep", bufs=1))
         psum = ctx.enter_context(tc.psum_pool(name="psum", bufs=1))
 
+        lists = {}
+
+        def load_list(name, src):
+            lists[name] = keep.tile([P, LIST_COLS], U16, name=name + "_list")
+            nc.sync.dma_start(lists[name][:], src)
+
         w1_raw = keep.tile([P, PACK, H], F32, name="w1_raw")
         nc.sync.dma_start(w1_raw[:], w1.rearrange("(p j) c -> p j c", j=PACK))
-        offs_t = keep.tile([P, LIST_COLS], U16, name="offs_t")
-        nc.sync.dma_start(offs_t[:], offs)
+        for name, src in (("offs", offs), ("n2", n2), ("n1", n1), ("n3", n3)):
+            load_list(name, src)
         x_tab = keep.tile([P, T], U32, name="x_tab")
         nc.sync.dma_start(x_tab[:].bitcast(I32), x_words[0].rearrange("p n t -> p (n t)").bitcast(I32))
 
@@ -51,12 +57,15 @@ def tile_picked_skipmxblerp_none_p_kernel(
                 s_tab[32 * q : 32 * q + 4, :].bitcast(I32), x_scales[0, 4 * q : 4 * q + 4, :].bitcast(I32)
             )
 
-        lists = {}
-        for name, src in (("n2", n2), ("n1", n1), ("n3", n3), ("n5", n5), ("n4", n4)):
-            lists[name] = keep.tile([P, LIST_COLS], U16, name=name + "_t")
-            nc.sync.dma_start(lists[name][:], src)
         w2_raw = keep.tile([P, PACK, N], F32, name="w2_raw")
         nc.sync.dma_start(w2_raw[:], w2.rearrange("(p j) c -> p j c", j=PACK))
+        for name, src in (("n5", n5), ("n4", n4)):
+            load_list(name, src)
+
+        y = []
+        for t in range(PACK):
+            y.append(keep.tile([P, 2 * S], F32, name="y%d" % t))
+            nc.vector.memset(y[t][:, S:], 0.0)
 
         cols = {}
         for name, src in (("gn", gn), ("sl", sl), ("th", th)):
@@ -64,12 +73,12 @@ def tile_picked_skipmxblerp_none_p_kernel(
             nc.gpsimd.dma_start(cols[name][:], src.rearrange("(p t) o -> p (t o)", t=PACK))
 
         xg_scales = keep.tile([P, S], U8, name="xg_scales", align_bytes=64)
-        nc.vector.tensor_copy(xg_scales[:], s_tab[:].indirect(offs_t[:]))
+        nc.vector.tensor_copy(xg_scales[:], s_tab[:].indirect(lists["offs"][:]))
 
         w1_bf = keep.tile([P, PACK * H], BF16, name="w1_bf", align_bytes=64)
         deal(nc.vector.tensor_copy, w1_bf, w1_raw, 0, W1_VECTOR_SHARE)
         deal(nc.scalar.copy, w1_bf, w1_raw, W1_VECTOR_SHARE, P)
-        w1_codes = keep.tile([P, H], U32, name="w1_codes", align_bytes=64)
+        w1_codes = keep.tile([P, H], U32, name="w1_codes", tag="w1_codes_w2_bf", align_bytes=64)
         w1_scales = keep.tile([P, H], U8, name="w1_scales", align_bytes=64)
         nc.vector.quantize_mx(out=w1_codes[:].bitcast(FP8X4), scales=w1_scales[:], in_=w1_bf[:])
 
@@ -79,107 +88,83 @@ def tile_picked_skipmxblerp_none_p_kernel(
         nc.gpsimd.tensor_scalar(bias[:], sl_th[:], -1.0, 0.0, ALU.mult, ALU.add)
 
         xg_words = keep.tile([P, S], U32, name="xg_words", align_bytes=64)
-        nc.vector.tensor_copy(xg_words[:], x_tab[:].indirect(offs_t[:]))
+        nc.vector.tensor_copy(xg_words[:], x_tab[:].indirect(lists["offs"][:]))
 
-        y = []
-        y_twin = []
-        for t in range(PACK):
-            y_bank = psum.tile([P, S], F32, name="y_bank%d" % t)
+        def product(bank, t, w_codes, w_scales, codes, scales):
             m_cols = slice(t * P, (t + 1) * P)
             nc.tensor.matmul_mx(
-                out=y_bank[:],
-                lhsT=w1_codes[:, m_cols].bitcast(FP8X4),
-                lhsT_scale=w1_scales[:, m_cols],
-                rhs=xg_words[:].bitcast(FP8X4),
-                rhs_scale=xg_scales[:],
+                out=bank[:],
+                lhsT=w_codes[:, m_cols].bitcast(FP8X4),
+                lhsT_scale=w_scales[:, m_cols],
+                rhs=codes[:].bitcast(FP8X4),
+                rhs_scale=scales[:],
                 start=True,
                 stop=True,
             )
-            y.append(keep.tile([P, S], F32, name="y%d" % t))
-            nc.vector.tensor_copy(y[t][:], y_bank[:])
-            y_twin.append(keep.tile([P, S], F32, name="y_twin%d" % t))
-            nc.sync.dma_start(y_twin[t][:], y[t][:])
 
-        w2_bf = keep.tile([P, PACK * N], BF16, name="w2_bf", align_bytes=64)
+        y_twin = keep.tile([P, PACK, S], F32, name="y_twin")
+        for t in range(PACK):
+            y_bank = psum.tile([P, S], F32, name="y_bank%d" % t)
+            product(y_bank, t, w1_codes, w1_scales, xg_words, xg_scales)
+            nc.vector.tensor_copy(y[t][:, :S], y_bank[:])
+            nc.sync.dma_start(y_twin[:, t, :], y[t][:, :S])
+
+        w2_bf = keep.tile([P, PACK * N], BF16, name="w2_bf", tag="w1_codes_w2_bf", align_bytes=64)
         deal(nc.vector.tensor_copy, w2_bf, w2_raw, 0, P)
         w2_codes = keep.tile([P, N], U32, name="w2_codes", align_bytes=64)
         w2_scales = keep.tile([P, N], U8, name="w2_scales", align_bytes=64)
         nc.vector.quantize_mx(out=w2_codes[:].bitcast(FP8X4), scales=w2_scales[:], in_=w2_bf[:])
 
-        def looked_up(t, name, half):
-            c0 = half * (LIST_COLS // 2)
-            return y[t][:].indirect(lists[name][:, c0 : c0 + LIST_COLS // 2])
+        def looked_up(t, name):
+            return y[t][:].indirect(lists[name][:])
 
-        def planes(name, half):
-            return keep.tile([P, PACK, HALF], F32, name="%s%d" % (name, half))
+        def planes(name):
+            return keep.tile([P, PACK, S], F32, name=name)
 
-        def second_product(half, gate_first):
-            pa, far, gate = planes("pa", half), planes("far", half), planes("gate", half)
-            for t in range(PACK):
-                if gate_first:
-                    nc.scalar.activation(gate[:, t, :], looked_up(t, "n2", half), ACT.Sigmoid)
-                nc.scalar.activation(pa[:, t, :], looked_up(t, "n1", half), ACT.Copy)
-                nc.scalar.activation(far[:, t, :], looked_up(t, "n3", half), ACT.Copy)
-            if not gate_first:
-                for t in range(PACK):
-                    nc.scalar.activation(gate[:, t, :], looked_up(t, "n2", half), ACT.Sigmoid)
-            step, z = planes("step", half), planes("z", half)
-            nc.vector.tensor_tensor(step[:], far[:], pa[:], ALU.subtract)
-            for t in range(PACK):
-                g = cols["gn"][:, t : t + 1]
-                nc.vector.scalar_tensor_tensor(far[:, t, :], step[:, t, :], g, gate[:, t, :], ALU.mult, ALU.mult)
-            for t in range(PACK):
-                g = cols["gn"][:, t : t + 1]
-                nc.vector.scalar_tensor_tensor(z[:, t, :], pa[:, t, :], g, far[:, t, :], ALU.mult, ALU.add)
-            z_bf = keep.tile([P, HALF * PACK], BF16, name="z_bf%d" % half, align_bytes=64)
+        far, gate, step, z = (planes(n) for n in ("far", "gate", "step", "z"))
+        diff = []
+
+        def skip(t, tag):
+            diff.append(keep.tile([P, S], F32, name="diff%d" % t, tag=tag, align_bytes=64))
+            nc.vector.tensor_tensor(diff[t][:], looked_up(t, "n5"), y_twin[:, t, :], ALU.subtract)
+
+        for t in range(PACK):
+            pa = keep.tile([P, S], F32, name="pa%d" % t, tag="pa_sg%d" % t)
+            if t == 0:
+                nc.scalar.activation(gate[:, t, :], looked_up(t, "n2"), ACT.Sigmoid)
+            nc.scalar.activation(pa[:], looked_up(t, "n1"), ACT.Copy)
+            nc.scalar.activation(far[:, t, :], looked_up(t, "n3"), ACT.Copy)
+            if t > 0:
+                nc.scalar.activation(gate[:, t, :], looked_up(t, "n2"), ACT.Sigmoid)
+            g = cols["gn"][:, t : t + 1]
+            nc.vector.tensor_tensor(step[:, t, :], far[:, t, :], pa[:], ALU.subtract)
+            nc.vector.scalar_tensor_tensor(far[:, t, :], step[:, t, :], g, gate[:, t, :], ALU.mult, ALU.mult)
+            nc.vector.scalar_tensor_tensor(z[:, t, :], pa[:], g, far[:, t, :], ALU.mult, ALU.add)
+            if t < PACK - 1:
+                skip(t, "diff%d" % t)
+
+        z_bf = keep.tile([P, S * PACK], BF16, name="z_bf", tag="z_bf_diff", align_bytes=64)
+        z_codes = keep.tile([P, S], U32, name="z_codes", align_bytes=64)
+        z_scales = keep.tile([P, S], U8, name="z_scales", align_bytes=64)
+        for half in range(2):
+            j_cols = slice(half * HALF, (half + 1) * HALF)
+            bf_cols = slice(half * HALF * PACK, (half + 1) * HALF * PACK)
             nc.vector.tensor_copy(
-                z_bf[:].rearrange("p (c i t) -> p c t i", i=4, t=PACK),
-                z[:].rearrange("p t (c i) -> p c t i", i=4),
+                z_bf[:, bf_cols].rearrange("p (c i t) -> p c t i", i=4, t=PACK),
+                z[:, :, j_cols].rearrange("p t (c i) -> p c t i", i=4),
             )
-            z_codes = keep.tile([P, HALF], U32, name="z_codes%d" % half, align_bytes=64)
-            z_scales = keep.tile([P, HALF], U8, name="z_scales%d" % half, align_bytes=64)
-            nc.vector.quantize_mx(out=z_codes[:].bitcast(FP8X4), scales=z_scales[:], in_=z_bf[:])
-            h_bank = psum.tile([P, PACK, HALF], F32, name="h_bank%d" % half)
-            for t in range(PACK):
-                m_cols = slice(t * P, (t + 1) * P)
-                nc.tensor.matmul_mx(
-                    out=h_bank[:, t, :],
-                    lhsT=w2_codes[:, m_cols].bitcast(FP8X4),
-                    lhsT_scale=w2_scales[:, m_cols],
-                    rhs=z_codes[:].bitcast(FP8X4),
-                    rhs_scale=z_scales[:],
-                    start=True,
-                    stop=True,
-                )
-            return h_bank
-
-        def skip(half):
-            diff = planes("diff", half)
-            for t in range(PACK):
-                nc.vector.tensor_tensor(
-                    diff[:, t, :], looked_up(t, "n5", half), y_twin[t][:, half * HALF : (half + 1) * HALF], ALU.subtract
-                )
-            return diff
+            nc.vector.quantize_mx(out=z_codes[:, j_cols].bitcast(FP8X4), scales=z_scales[:, j_cols], in_=z_bf[:, bf_cols])
+        skip(PACK - 1, "z_bf_diff")
 
         out_v = out.rearrange("(p t) j -> p t j", t=PACK)
-
-        def finish(half, h_bank, diff, pieces):
-            sg = planes("sg", half)
-            for t in range(PACK):
-                nc.scalar.activation(
-                    sg[:, t, :], looked_up(t, "n4", half), ACT.Sigmoid,
-                    bias=bias[:, t : t + 1], scale=cols["sl"][:, t : t + 1],
-                )
-            gated, res = planes("gated", half), planes("res", half)
-            for piece in pieces:
-                nc.vector.tensor_tensor(gated[:, piece, :], h_bank[:, piece, :], sg[:, piece, :], ALU.mult)
-            for piece in pieces:
-                nc.vector.tensor_tensor(res[:, piece, :], gated[:, piece, :], diff[:, piece, :], ALU.max)
-                nc.sync.dma_start(out_v[:, piece, half * HALF : (half + 1) * HALF], res[:, piece, :])
-
-        h0 = second_product(0, True)
-        d0 = skip(0)
-        h1 = second_product(1, False)
-        d1 = skip(1)
-        finish(0, h0, d0, [slice(0, 4)])
-        finish(1, h1, d1, [slice(0, 2), slice(2, 4)])
+        gated, res = planes("gated"), planes("res")
+        for t in range(PACK):
+            sg = keep.tile([P, S], F32, name="sg%d" % t, tag="pa_sg%d" % t)
+            nc.scalar.activation(
+                sg[:], looked_up(t, "n4"), ACT.Sigmoid, bias=bias[:, t : t + 1], scale=cols["sl"][:, t : t + 1]
+            )
+            h_bank = psum.tile([P, S], F32, name="h_bank%d" % t)
+            product(h_bank, t, w2_codes, w2_scales, z_codes, z_scales)
+            nc.vector.tensor_tensor(gated[:, t, :], h_bank[:], sg[:], ALU.mult)
+            nc.vector.tensor_tensor(res[:, t, :], gated[:, t, :], diff[t][:], ALU.max)
+            nc.sync.dma_start(out_v[:, t, :], res[:, t, :])

@@ -20,12 +20,15 @@ PACK = 4
 HALF = S // 2
 LIST_COLS = S // 16
 W1_VECTOR_SHARE = 88
+FUSED = 3
+W2_FIRST = 256
 
 
-def deal(engine_copy, grouped, raw, m0, m1):
+def deal(engine_copy, grouped, m0, raw):
+    m1 = m0 + raw.shape[2] // PACK
     engine_copy(
         grouped[:].rearrange("p (t m j) -> p m j t", t=PACK, j=PACK)[:, m0:m1],
-        raw[:].rearrange("p j (m t) -> p m j t", t=PACK)[:, m0:m1],
+        raw.rearrange("p j (m t) -> p m j t", t=PACK),
     )
 
 
@@ -43,24 +46,35 @@ def tile_picked_skipmxblerp_none_p_kernel(
             lists[name] = keep.tile([P, LIST_COLS], U16, name=name + "_list")
             nc.sync.dma_start(lists[name][:], src)
 
+        s_rows = keep.tile([P, T], U8, name="s_rows")
+        for q in range(4):
+            nc.sync.dma_start(
+                s_rows[32 * q : 32 * q + 4, :].bitcast(I32), x_scales[0, 4 * q : 4 * q + 4, :].bitcast(I32)
+            )
+        load_list("offs", offs)
         w1_raw = keep.tile([P, PACK, H], F32, name="w1_raw")
         nc.sync.dma_start(w1_raw[:], w1.rearrange("(p j) c -> p j c", j=PACK))
-        for name, src in (("offs", offs), ("n2", n2), ("n1", n1), ("n3", n3)):
-            load_list(name, src)
         x_tab = keep.tile([P, T], U32, name="x_tab")
         nc.sync.dma_start(x_tab[:].bitcast(I32), x_words[0].rearrange("p n t -> p (n t)").bitcast(I32))
+
+
+        for name, src in (("n2", n2), ("n1", n1), ("n3", n3)):
+            load_list(name, src)
+        w2_rows = w2.rearrange("(p j) c -> p j c", j=PACK)
+        w2_raw = []
+        for part, c_cols in enumerate((slice(0, W2_FIRST), slice(W2_FIRST, N))):
+            width = c_cols.stop - c_cols.start
+            name = "w2_raw%d" % part
+            w2_raw.append(keep.tile([P, PACK, width], F32, name=name, tag=name, align_bytes=64))
+            nc.sync.dma_start(w2_raw[part][:], w2_rows[:, :, c_cols])
+        for name, src in (("n5", n5), ("n4", n4)):
+            load_list(name, src)
 
         s_tab = keep.tile([P, T], U8, name="s_tab")
         nc.vector.memset(s_tab[:].bitcast(I32), 0)
         for q in range(4):
-            nc.scalar.dma_start(
-                s_tab[32 * q : 32 * q + 4, :].bitcast(I32), x_scales[0, 4 * q : 4 * q + 4, :].bitcast(I32)
-            )
-
-        w2_raw = keep.tile([P, PACK, N], F32, name="w2_raw")
-        nc.sync.dma_start(w2_raw[:], w2.rearrange("(p j) c -> p j c", j=PACK))
-        for name, src in (("n5", n5), ("n4", n4)):
-            load_list(name, src)
+            rows = slice(32 * q, 32 * q + 4)
+            nc.vector.tensor_copy(s_tab[rows, :].bitcast(I32), s_rows[rows, :].bitcast(I32))
 
         y = []
         for t in range(PACK):
@@ -76,9 +90,9 @@ def tile_picked_skipmxblerp_none_p_kernel(
         nc.vector.tensor_copy(xg_scales[:], s_tab[:].indirect(lists["offs"][:]))
 
         w1_bf = keep.tile([P, PACK * H], BF16, name="w1_bf", align_bytes=64)
-        deal(nc.vector.tensor_copy, w1_bf, w1_raw, 0, W1_VECTOR_SHARE)
-        deal(nc.scalar.copy, w1_bf, w1_raw, W1_VECTOR_SHARE, P)
-        w1_codes = keep.tile([P, H], U32, name="w1_codes", tag="w1_codes_w2_bf", align_bytes=64)
+        deal(nc.vector.tensor_copy, w1_bf, 0, w1_raw[:, :, : PACK * W1_VECTOR_SHARE])
+        deal(nc.scalar.copy, w1_bf, W1_VECTOR_SHARE, w1_raw[:, :, PACK * W1_VECTOR_SHARE :])
+        w1_codes = keep.tile([P, H], U32, name="w1_codes", align_bytes=64)
         w1_scales = keep.tile([P, H], U8, name="w1_scales", align_bytes=64)
         nc.vector.quantize_mx(out=w1_codes[:].bitcast(FP8X4), scales=w1_scales[:], in_=w1_bf[:])
 
@@ -102,69 +116,85 @@ def tile_picked_skipmxblerp_none_p_kernel(
                 stop=True,
             )
 
-        y_twin = keep.tile([P, PACK, S], F32, name="y_twin")
+        y_twin = [keep.tile([P, S], F32, name="y_twin%d" % t, tag="y_twin%d" % t, align_bytes=64) for t in range(FUSED)]
         for t in range(PACK):
             y_bank = psum.tile([P, S], F32, name="y_bank%d" % t)
             product(y_bank, t, w1_codes, w1_scales, xg_words, xg_scales)
             nc.vector.tensor_copy(y[t][:, :S], y_bank[:])
-            nc.sync.dma_start(y_twin[:, t, :], y[t][:, :S])
+            if t < FUSED:
+                nc.sync.dma_start(y_twin[t][:], y[t][:, :S])
 
-        w2_bf = keep.tile([P, PACK * N], BF16, name="w2_bf", tag="w1_codes_w2_bf", align_bytes=64)
-        deal(nc.vector.tensor_copy, w2_bf, w2_raw, 0, P)
+        w2_bf = keep.tile([P, PACK * N], BF16, name="w2_bf", tag="w2_bf", align_bytes=64)
+        deal(nc.vector.tensor_copy, w2_bf, 0, w2_raw[0][:])
+        deal(nc.vector.tensor_copy, w2_bf, W2_FIRST // PACK, w2_raw[1][:])
         w2_codes = keep.tile([P, N], U32, name="w2_codes", align_bytes=64)
         w2_scales = keep.tile([P, N], U8, name="w2_scales", align_bytes=64)
         nc.vector.quantize_mx(out=w2_codes[:].bitcast(FP8X4), scales=w2_scales[:], in_=w2_bf[:])
 
-        def looked_up(t, name):
-            return y[t][:].indirect(lists[name][:])
+        def looked_up(t, name, j_cols=slice(0, S)):
+            return y[t][:].indirect(lists[name][:, j_cols.start // 16 : j_cols.stop // 16])
 
         def planes(name):
             return keep.tile([P, PACK, S], F32, name=name)
 
-        far, gate, step, z = (planes(n) for n in ("far", "gate", "step", "z"))
-        diff = []
+        def row_tile(name, t, tag=None):
+            return keep.tile([P, S], F32, name="%s%d" % (name, t), tag=tag or "%s%d" % (name, t), align_bytes=64)
 
-        def skip(t, tag):
-            diff.append(keep.tile([P, S], F32, name="diff%d" % t, tag=tag, align_bytes=64))
-            nc.vector.tensor_tensor(diff[t][:], looked_up(t, "n5"), y_twin[:, t, :], ALU.subtract)
-
+        step_slots = ["w2_bf", "y_twin0", "y_twin1", "pa2"]
+        halves = [slice(0, HALF), slice(HALF, S)]
+        gate, z = planes("gate"), planes("z")
+        diff = {}
         for t in range(PACK):
-            pa = keep.tile([P, S], F32, name="pa%d" % t, tag="pa_sg%d" % t)
+            pa, far = row_tile("pa", t), row_tile("far", t)
+            pair = keep.tile([P, 2 if t < FUSED else 1, S], F32, name="pair%d" % t, tag=step_slots[t], align_bytes=64)
+            step = pair[:, 0, :]
+            pieces = halves if t == PACK - 1 else [slice(0, S)]
             if t == 0:
                 nc.scalar.activation(gate[:, t, :], looked_up(t, "n2"), ACT.Sigmoid)
             nc.scalar.activation(pa[:], looked_up(t, "n1"), ACT.Copy)
-            nc.scalar.activation(far[:, t, :], looked_up(t, "n3"), ACT.Copy)
+            nc.scalar.activation(far[:], looked_up(t, "n3"), ACT.Copy)
             if t > 0:
-                nc.scalar.activation(gate[:, t, :], looked_up(t, "n2"), ACT.Sigmoid)
+                for j_cols in pieces:
+                    nc.scalar.activation(gate[:, t, j_cols], looked_up(t, "n2", j_cols), ACT.Sigmoid)
             g = cols["gn"][:, t : t + 1]
-            nc.vector.tensor_tensor(step[:, t, :], far[:, t, :], pa[:], ALU.subtract)
-            nc.vector.scalar_tensor_tensor(far[:, t, :], step[:, t, :], g, gate[:, t, :], ALU.mult, ALU.mult)
-            nc.vector.scalar_tensor_tensor(z[:, t, :], pa[:], g, far[:, t, :], ALU.mult, ALU.add)
-            if t < PACK - 1:
-                skip(t, "diff%d" % t)
+            nc.vector.tensor_tensor(step, far[:], pa[:], ALU.subtract)
+            for j_cols in pieces:
+                nc.vector.scalar_tensor_tensor(far[:, j_cols], step[:, j_cols], g, gate[:, t, j_cols], ALU.mult, ALU.mult)
+                nc.vector.scalar_tensor_tensor(z[:, t, j_cols], pa[:, j_cols], g, far[:, j_cols], ALU.mult, ALU.add)
+            if t < FUSED:
+                diff[t] = pair[:, 1, :]
+                nc.vector.tensor_tensor(diff[t], looked_up(t, "n5"), y_twin[t][:], ALU.subtract)
 
-        z_bf = keep.tile([P, S * PACK], BF16, name="z_bf", tag="z_bf_diff", align_bytes=64)
+        z_bf = keep.tile([P, S * PACK], BF16, name="z_bf", tag="z_bf", align_bytes=64)
         z_codes = keep.tile([P, S], U32, name="z_codes", align_bytes=64)
         z_scales = keep.tile([P, S], U8, name="z_scales", align_bytes=64)
-        for half in range(2):
-            j_cols = slice(half * HALF, (half + 1) * HALF)
-            bf_cols = slice(half * HALF * PACK, (half + 1) * HALF * PACK)
+        for j_cols in halves:
+            bf_cols = slice(j_cols.start * PACK, j_cols.stop * PACK)
             nc.vector.tensor_copy(
                 z_bf[:, bf_cols].rearrange("p (c i t) -> p c t i", i=4, t=PACK),
                 z[:, :, j_cols].rearrange("p t (c i) -> p c t i", i=4),
             )
             nc.vector.quantize_mx(out=z_codes[:, j_cols].bitcast(FP8X4), scales=z_scales[:, j_cols], in_=z_bf[:, bf_cols])
-        skip(PACK - 1, "z_bf_diff")
+
+        freed = ["pa1", "y_twin2", "far2", "pa2", "pa3"]
+        sg = []
+        for kind, t in (("n5", 3), ("n4", 0), ("n4", 1), ("n4", 2), ("n4", 3)):
+            fetched = row_tile(kind, t, tag=freed.pop(0))
+            if kind == "n5":
+                nc.scalar.activation(fetched[:], looked_up(t, "n5"), ACT.Copy)
+                diff[t] = row_tile("diff", t, tag="z_bf")[:]
+                nc.vector.tensor_tensor(diff[t], fetched[:], y[t][:, :S], ALU.subtract)
+            else:
+                nc.scalar.activation(
+                    fetched[:], looked_up(t, "n4"), ACT.Sigmoid, bias=bias[:, t : t + 1], scale=cols["sl"][:, t : t + 1]
+                )
+                sg.append(fetched)
 
         out_v = out.rearrange("(p t) j -> p t j", t=PACK)
         gated, res = planes("gated"), planes("res")
         for t in range(PACK):
-            sg = keep.tile([P, S], F32, name="sg%d" % t, tag="pa_sg%d" % t)
-            nc.scalar.activation(
-                sg[:], looked_up(t, "n4"), ACT.Sigmoid, bias=bias[:, t : t + 1], scale=cols["sl"][:, t : t + 1]
-            )
             h_bank = psum.tile([P, S], F32, name="h_bank%d" % t)
             product(h_bank, t, w2_codes, w2_scales, z_codes, z_scales)
-            nc.vector.tensor_tensor(gated[:, t, :], h_bank[:], sg[:], ALU.mult)
-            nc.vector.tensor_tensor(res[:, t, :], gated[:, t, :], diff[t][:], ALU.max)
+            nc.vector.tensor_tensor(gated[:, t, :], h_bank[:], sg[t][:], ALU.mult)
+            nc.vector.tensor_tensor(res[:, t, :], gated[:, t, :], diff[t], ALU.max)
             nc.sync.dma_start(out_v[:, t, :], res[:, t, :])

@@ -20,15 +20,15 @@ PACK = 4
 HALF = S // 2
 LIST_COLS = S // 16
 W1_VECTOR_SHARE = 88
-FUSED = 3
+FUSED = 2
 W2_FIRST = 256
 
 
 def deal(engine_copy, grouped, m0, raw):
     m1 = m0 + raw.shape[2] // PACK
     engine_copy(
-        grouped[:].rearrange("p (t m j) -> p m j t", t=PACK, j=PACK)[:, m0:m1],
-        raw.rearrange("p j (m t) -> p m j t", t=PACK),
+        grouped[:].rearrange("p (t m j) -> p m t j", t=PACK, j=PACK)[:, m0:m1],
+        raw.rearrange("p j (m t) -> p m t j", t=PACK),
     )
 
 
@@ -176,13 +176,14 @@ def tile_picked_skipmxblerp_none_p_kernel(
             )
             nc.vector.quantize_mx(out=z_codes[:, j_cols].bitcast(FP8X4), scales=z_scales[:, j_cols], in_=z_bf[:, bf_cols])
 
-        freed = ["pa1", "y_twin2", "far2", "pa2", "pa3"]
+        freed = ["pa1", "y_twin1", "far2", "pa2", "pa3", "far3"]
         sg = []
-        for kind, t in (("n5", 3), ("n4", 0), ("n4", 1), ("n4", 2), ("n4", 3)):
+        late_diff = keep.tile([P, PACK - FUSED, S], F32, name="late_diff", tag="z_bf", align_bytes=64)
+        for kind, t in (("n5", 2), ("n5", 3), ("n4", 0), ("n4", 1), ("n4", 2), ("n4", 3)):
             fetched = row_tile(kind, t, tag=freed.pop(0))
             if kind == "n5":
                 nc.scalar.activation(fetched[:], looked_up(t, "n5"), ACT.Copy)
-                diff[t] = row_tile("diff", t, tag="z_bf")[:]
+                diff[t] = late_diff[:, t - FUSED, :]
                 nc.vector.tensor_tensor(diff[t], fetched[:], y[t][:, :S], ALU.subtract)
             else:
                 nc.scalar.activation(

@@ -89,7 +89,7 @@ def tile_picked_skipmxblerp_none_p_kernel(
         xg_scales = keep.tile([P, S], U8, name="xg_scales", align_bytes=64)
         nc.vector.tensor_copy(xg_scales[:], s_tab[:].indirect(lists["offs"][:]))
 
-        w1_bf = keep.tile([P, PACK * H], BF16, name="w1_bf", align_bytes=64)
+        w1_bf = keep.tile([P, PACK * H], BF16, name="w1_bf", tag="w1_bf", align_bytes=64)
         deal(nc.vector.tensor_copy, w1_bf, 0, w1_raw[:, :, : PACK * W1_VECTOR_SHARE])
         deal(nc.scalar.copy, w1_bf, W1_VECTOR_SHARE, w1_raw[:, :, PACK * W1_VECTOR_SHARE :])
         w1_codes = keep.tile([P, H], U32, name="w1_codes", align_bytes=64)
@@ -101,26 +101,32 @@ def tile_picked_skipmxblerp_none_p_kernel(
         nc.gpsimd.tensor_tensor(sl_th[:], cols["sl"][:], cols["th"][:], ALU.mult)
         nc.gpsimd.tensor_scalar(bias[:], sl_th[:], -1.0, 0.0, ALU.mult, ALU.add)
 
-        xg_words = keep.tile([P, S], U32, name="xg_words", align_bytes=64)
-        nc.vector.tensor_copy(xg_words[:], x_tab[:].indirect(lists["offs"][:]))
+        xg_words = keep.tile([P, S], U32, name="xg_words", tag="w1_bf", align_bytes=64)
+        halves = [slice(0, HALF), slice(HALF, S)]
+        for j_cols in halves:
+            nc.vector.tensor_copy(
+                xg_words[:, j_cols], x_tab[:].indirect(lists["offs"][:, j_cols.start // 16 : j_cols.stop // 16])
+            )
 
         def product(bank, t, w_codes, w_scales, codes, scales):
             m_cols = slice(t * P, (t + 1) * P)
             nc.tensor.matmul_mx(
-                out=bank[:],
+                out=bank,
                 lhsT=w_codes[:, m_cols].bitcast(FP8X4),
                 lhsT_scale=w_scales[:, m_cols],
-                rhs=codes[:].bitcast(FP8X4),
-                rhs_scale=scales[:],
+                rhs=codes.bitcast(FP8X4),
+                rhs_scale=scales,
                 start=True,
                 stop=True,
             )
 
         y_twin = [keep.tile([P, S], F32, name="y_twin%d" % t, tag="y_twin%d" % t, align_bytes=64) for t in range(FUSED)]
         for t in range(PACK):
-            y_bank = psum.tile([P, S], F32, name="y_bank%d" % t)
-            product(y_bank, t, w1_codes, w1_scales, xg_words, xg_scales)
-            nc.vector.tensor_copy(y[t][:, :S], y_bank[:])
+            for j_cols in halves if t == 0 else [slice(0, S)]:
+                name = "y_bank%d_%d" % (t, j_cols.start)
+                y_bank = psum.tile([P, j_cols.stop - j_cols.start], F32, name=name, tag=name)
+                product(y_bank[:], t, w1_codes, w1_scales, xg_words[:, j_cols], xg_scales[:, j_cols])
+                nc.vector.tensor_copy(y[t][:, j_cols], y_bank[:])
             if t < FUSED:
                 nc.sync.dma_start(y_twin[t][:], y[t][:, :S])
 
@@ -141,7 +147,6 @@ def tile_picked_skipmxblerp_none_p_kernel(
             return keep.tile([P, S], F32, name="%s%d" % (name, t), tag=tag or "%s%d" % (name, t), align_bytes=64)
 
         step_slots = ["w2_bf", "y_twin0", "y_twin1", "pa2"]
-        halves = [slice(0, HALF), slice(HALF, S)]
         gate, z = planes("gate"), planes("z")
         diff = {}
         for t in range(PACK):
@@ -194,8 +199,13 @@ def tile_picked_skipmxblerp_none_p_kernel(
         out_v = out.rearrange("(p t) j -> p t j", t=PACK)
         gated, res = planes("gated"), planes("res")
         for t in range(PACK):
-            h_bank = psum.tile([P, S], F32, name="h_bank%d" % t)
-            product(h_bank, t, w2_codes, w2_scales, z_codes, z_scales)
-            nc.vector.tensor_tensor(gated[:, t, :], h_bank[:], sg[t][:], ALU.mult)
-            nc.vector.tensor_tensor(res[:, t, :], gated[:, t, :], diff[t], ALU.max)
-            nc.sync.dma_start(out_v[:, t, :], res[:, t, :])
+            name = "y_bank%d_0" % t
+            h_bank = psum.tile([P, S], F32, name="h_bank%d" % t, tag=name)
+            product(h_bank[:], t, w2_codes, w2_scales, z_codes[:], z_scales[:])
+            pieces = halves if t == PACK - 1 else [slice(0, S)]
+            for j_cols in pieces:
+                nc.vector.tensor_tensor(gated[:, t, j_cols], h_bank[:, j_cols], sg[t][:, j_cols], ALU.mult)
+            for j_cols in pieces:
+                nc.vector.tensor_tensor(res[:, t, j_cols], gated[:, t, j_cols], diff[t][:, j_cols], ALU.max)
+                queue = nc.scalar if j_cols.start else nc.sync
+                queue.dma_start(out_v[:, t, j_cols], res[:, t, j_cols])

from contextlib import ExitStack

import concourse.mybir as mybir

K, T, S, H, N = 512, 2048, 256, 512, 512
FLOPS = 2 * K * H * S + 2 * H * N * S

F32 = mybir.dt.float32
BF16 = mybir.dt.bfloat16
I32 = mybir.dt.int32
U32 = mybir.dt.uint32
U16 = mybir.dt.uint16
U8 = mybir.dt.uint8
FP8X4 = mybir.dt.float8_e4m3fn_x4
ALU = mybir.AluOpType
ACT = mybir.ActivationFunctionType

P = 128
PACK = 4
HALF = S // 2
LIST_COLS = S // 16
W1_VECTOR_SHARE = 88
FUSED = 2
W2_FIRST = 256


def deal(engine_copy, grouped, m0, raw):
    m1 = m0 + raw.shape[2] // PACK
    engine_copy(
        grouped[:].rearrange("p (t m j) -> p m t j", t=PACK, j=PACK)[:, m0:m1],
        raw.rearrange("p j (m t) -> p m t j", t=PACK),
    )


def tile_picked_skipmxblerp_none_p_kernel(
    tc, x_words, x_scales, w1, gn, w2, sl, th, offs, n1, n2, n3, n4, n5, out
):
    nc = tc.nc
    with ExitStack() as ctx:
        keep = ctx.enter_context(tc.tile_pool(name="keep", bufs=1))
        psum = ctx.enter_context(tc.psum_pool(name="psum", bufs=1))

        lists = {}

        def load_list(name, src):
            lists[name] = keep.tile([P, LIST_COLS], U16, name=name + "_list")
            nc.sync.dma_start(lists[name][:], src)

        s_rows = keep.tile([P, T], U8, name="s_rows")
        for q in range(4):
            nc.sync.dma_start(
                s_rows[32 * q : 32 * q + 4, :].bitcast(I32), x_scales[0, 4 * q : 4 * q + 4, :].bitcast(I32)
            )
        load_list("offs", offs)
        w1_raw = keep.tile([P, PACK, H], F32, name="w1_raw")
        nc.sync.dma_start(w1_raw[:], w1.rearrange("(p j) c -> p j c", j=PACK))
        x_tab = keep.tile([P, T], U32, name="x_tab")
        nc.sync.dma_start(x_tab[:].bitcast(I32), x_words[0].rearrange("p n t -> p (n t)").bitcast(I32))


        for name, src in (("n2", n2), ("n1", n1), ("n3", n3)):
            load_list(name, src)
        w2_rows = w2.rearrange("(p j) c -> p j c", j=PACK)
        w2_raw = []
        for part, c_cols in enumerate((slice(0, W2_FIRST), slice(W2_FIRST, N))):
            width = c_cols.stop - c_cols.start
            name = "w2_raw%d" % part
            w2_raw.append(keep.tile([P, PACK, width], F32, name=name, tag=name, align_bytes=64))
            nc.sync.dma_start(w2_raw[part][:], w2_rows[:, :, c_cols])
        for name, src in (("n5", n5), ("n4", n4)):
            load_list(name, src)

        s_tab = keep.tile([P, T], U8, name="s_tab")
        nc.vector.memset(s_tab[:].bitcast(I32), 0)
        for q in range(4):
            rows = slice(32 * q, 32 * q + 4)
            nc.vector.tensor_copy(s_tab[rows, :].bitcast(I32), s_rows[rows, :].bitcast(I32))

        y = []
        for t in range(PACK):
            y.append(keep.tile([P, 2 * S], F32, name="y%d" % t))
            nc.vector.memset(y[t][:, S:], 0.0)

        cols = {}
        for name, src in (("gn", gn), ("sl", sl), ("th", th)):
            cols[name] = keep.tile([P, PACK], F32, name=name + "_t")
            nc.gpsimd.dma_start(cols[name][:], src.rearrange("(p t) o -> p (t o)", t=PACK))

        xg_scales = keep.tile([P, S], U8, name="xg_scales", align_bytes=64)
        nc.vector.tensor_copy(xg_scales[:], s_tab[:].indirect(lists["offs"][:]))

        w1_bf = keep.tile([P, PACK * H], BF16, name="w1_bf", tag="w1_bf", align_bytes=64)
        deal(nc.vector.tensor_copy, w1_bf, 0, w1_raw[:, :, : PACK * W1_VECTOR_SHARE])
        deal(nc.scalar.copy, w1_bf, W1_VECTOR_SHARE, w1_raw[:, :, PACK * W1_VECTOR_SHARE :])
        w1_codes = keep.tile([P, H], U32, name="w1_codes", align_bytes=64)
        w1_scales = keep.tile([P, H], U8, name="w1_scales", align_bytes=64)
        nc.vector.quantize_mx(out=w1_codes[:].bitcast(FP8X4), scales=w1_scales[:], in_=w1_bf[:])

        bias = keep.tile([P, PACK], F32, name="bias")
        sl_th = keep.tile([P, PACK], F32, name="sl_th")
        nc.gpsimd.tensor_tensor(sl_th[:], cols["sl"][:], cols["th"][:], ALU.mult)
        nc.gpsimd.tensor_scalar(bias[:], sl_th[:], -1.0, 0.0, ALU.mult, ALU.add)

        xg_words = keep.tile([P, S], U32, name="xg_words", tag="w1_bf", align_bytes=64)
        halves = [slice(0, HALF), slice(HALF, S)]
        for j_cols in halves:
            nc.vector.tensor_copy(
                xg_words[:, j_cols], x_tab[:].indirect(lists["offs"][:, j_cols.start // 16 : j_cols.stop // 16])
            )

        def product(bank, t, w_codes, w_scales, codes, scales):
            m_cols = slice(t * P, (t + 1) * P)
            nc.tensor.matmul_mx(
                out=bank,
                lhsT=w_codes[:, m_cols].bitcast(FP8X4),
                lhsT_scale=w_scales[:, m_cols],
                rhs=codes.bitcast(FP8X4),
                rhs_scale=scales,
                start=True,
                stop=True,
            )

        y_twin = [keep.tile([P, S], F32, name="y_twin%d" % t, tag="y_twin%d" % t, align_bytes=64) for t in range(FUSED)]
        for t in range(PACK):
            for j_cols in halves if t == 0 else [slice(0, S)]:
                name = "y_bank%d_%d" % (t, j_cols.start)
                y_bank = psum.tile([P, j_cols.stop - j_cols.start], F32, name=name, tag=name)
                product(y_bank[:], t, w1_codes, w1_scales, xg_words[:, j_cols], xg_scales[:, j_cols])
                nc.vector.tensor_copy(y[t][:, j_cols], y_bank[:])
            if t < FUSED:
                nc.sync.dma_start(y_twin[t][:], y[t][:, :S])

        w2_bf = keep.tile([P, PACK * N], BF16, name="w2_bf", tag="w2_bf", align_bytes=64)
        deal(nc.vector.tensor_copy, w2_bf, 0, w2_raw[0][:])
        deal(nc.vector.tensor_copy, w2_bf, W2_FIRST // PACK, w2_raw[1][:])
        w2_codes = keep.tile([P, N], U32, name="w2_codes", align_bytes=64)
        w2_scales = keep.tile([P, N], U8, name="w2_scales", align_bytes=64)
        nc.vector.quantize_mx(out=w2_codes[:].bitcast(FP8X4), scales=w2_scales[:], in_=w2_bf[:])

        def looked_up(t, name, j_cols=slice(0, S)):
            return y[t][:].indirect(lists[name][:, j_cols.start // 16 : j_cols.stop // 16])

        def planes(name):
            return keep.tile([P, PACK, S], F32, name=name)

        def row_tile(name, t, tag=None):
            return keep.tile([P, S], F32, name="%s%d" % (name, t), tag=tag or "%s%d" % (name, t), align_bytes=64)

        step_slots = ["w2_bf", "y_twin0", "y_twin1", "pa2"]
        gate, z = planes("gate"), planes("z")
        diff = {}
        for t in range(PACK):
            pa, far = row_tile("pa", t), row_tile("far", t)
            pair = keep.tile([P, 2 if t < FUSED else 1, S], F32, name="pair%d" % t, tag=step_slots[t], align_bytes=64)
            step = pair[:, 0, :]
            pieces = halves if t == PACK - 1 else [slice(0, S)]
            if t == 0:
                nc.scalar.activation(gate[:, t, :], looked_up(t, "n2"), ACT.Sigmoid)
            nc.scalar.activation(pa[:], looked_up(t, "n1"), ACT.Copy)
            nc.scalar.activation(far[:], looked_up(t, "n3"), ACT.Copy)
            if t > 0:
                for j_cols in pieces:
                    nc.scalar.activation(gate[:, t, j_cols], looked_up(t, "n2", j_cols), ACT.Sigmoid)
            g = cols["gn"][:, t : t + 1]
            nc.vector.tensor_tensor(step, far[:], pa[:], ALU.subtract)
            for j_cols in pieces:
                nc.vector.scalar_tensor_tensor(far[:, j_cols], step[:, j_cols], g, gate[:, t, j_cols], ALU.mult, ALU.mult)
                nc.vector.scalar_tensor_tensor(z[:, t, j_cols], pa[:, j_cols], g, far[:, j_cols], ALU.mult, ALU.add)
            if t < FUSED:
                diff[t] = pair[:, 1, :]
                nc.vector.tensor_tensor(diff[t], looked_up(t, "n5"), y_twin[t][:], ALU.subtract)

        z_bf = keep.tile([P, S * PACK], BF16, name="z_bf", tag="z_bf", align_bytes=64)
        z_codes = keep.tile([P, S], U32, name="z_codes", align_bytes=64)
        z_scales = keep.tile([P, S], U8, name="z_scales", align_bytes=64)
        for j_cols in halves:
            bf_cols = slice(j_cols.start * PACK, j_cols.stop * PACK)
            nc.vector.tensor_copy(
                z_bf[:, bf_cols].rearrange("p (c i t) -> p c t i", i=4, t=PACK),
                z[:, :, j_cols].rearrange("p t (c i) -> p c t i", i=4),
            )
            nc.vector.quantize_mx(out=z_codes[:, j_cols].bitcast(FP8X4), scales=z_scales[:, j_cols], in_=z_bf[:, bf_cols])

        freed = ["pa1", "y_twin1", "far2", "pa2", "pa3", "far3"]
        sg = []
        late_diff = keep.tile([P, PACK - FUSED, S], F32, name="late_diff", tag="z_bf", align_bytes=64)
        for kind, t in (("n5", 2), ("n5", 3), ("n4", 0), ("n4", 1), ("n4", 2), ("n4", 3)):
            fetched = row_tile(kind, t, tag=freed.pop(0))
            if kind == "n5":
                nc.scalar.activation(fetched[:], looked_up(t, "n5"), ACT.Copy)
                diff[t] = late_diff[:, t - FUSED, :]
                nc.vector.tensor_tensor(diff[t], fetched[:], y[t][:, :S], ALU.subtract)
            else:
                nc.scalar.activation(
                    fetched[:], looked_up(t, "n4"), ACT.Sigmoid, bias=bias[:, t : t + 1], scale=cols["sl"][:, t : t + 1]
                )
                sg.append(fetched)

        out_v = out.rearrange("(p t) j -> p t j", t=PACK)
        gated, res = planes("gated"), planes("res")
        for t in range(PACK):
            name = "y_bank%d_0" % t
            h_bank = psum.tile([P, S], F32, name="h_bank%d" % t, tag=name)
            product(h_bank[:], t, w2_codes, w2_scales, z_codes[:], z_scales[:])
            pieces = halves if t == PACK - 1 else [slice(0, S)]
            for j_cols in pieces:
                nc.vector.tensor_tensor(gated[:, t, j_cols], h_bank[:, j_cols], sg[t][:, j_cols], ALU.mult)
            for j_cols in pieces:
                nc.vector.tensor_tensor(res[:, t, j_cols], gated[:, t, j_cols], diff[t][:, j_cols], ALU.max)
                queue = nc.scalar if j_cols.start else nc.sync
                queue.dma_start(out_v[:, t, j_cols], res[:, t, j_cols])
